import numpy as np
import ml_dtypes


def mxq(x, axis, fmt="e4m3"):
    dtype, down = {"e4m3": (ml_dtypes.float8_e4m3fn, 7), "e5m2": (ml_dtypes.float8_e5m2, 14)}[fmt]
    v = np.moveaxis(np.asarray(x, np.float32).astype(ml_dtypes.bfloat16).astype(np.float64), axis, -1)
    blocks = v.reshape(v.shape[:-1] + (-1, 32))
    amax = np.abs(blocks).max(-1, keepdims=True)
    byte = np.maximum(np.where(amax > 0, np.frexp(amax)[1] - 1 + 127, 0) - down, 1)
    scale = np.exp2(byte - 127.0)
    codes = (blocks / scale).astype(np.float32).astype(dtype).astype(np.float64)
    return np.moveaxis((codes * scale).reshape(v.shape), -1, axis)


WIDE = False


def mx_kscale(k):
    if not WIDE:
        return np.ones(k)
    levels = np.array([10, -10, 5, -5, 0])
    if k % 512:
        return np.exp2(np.random.permutation(np.resize(levels, k // 32))).repeat(32)
    a = np.empty((k // 512, 16))
    for p in range(k // 512):
        a[p, :8] = np.random.permutation(np.resize(levels, 8))
        for g in range(8):
            far = levels[np.abs(levels - a[p, g]) >= 10]
            a[p, g + 8] = far[np.random.randint(len(far))]
    return np.exp2(a.ravel()).repeat(32)


def f64(x):
    return np.asarray(x).astype(np.float64)


def striped(idx):
    return np.tile(idx.reshape(-1, 16).T, (8, 1)).astype(np.uint16)


def unstriped(offs):
    return offs[:16].T.reshape(-1).astype(np.int64)


E2M1 = np.array([0.0, 0.5, 1.0, 1.5, 2.0, 3.0, 4.0, 6.0, -0.0, -0.5, -1.0, -1.5, -2.0, -3.0, -4.0, -6.0])


def pack_weight(w, fmt):
    k, n = w.shape
    w = f64(np.asarray(w, np.float32).astype(ml_dtypes.bfloat16)).reshape(k // 32, 32, n)
    amax = np.abs(w).max(1)
    if fmt == "e4m3":
        byte = np.frexp(amax)[1] - 1 + 127 - 7
    else:
        mant, ex = np.frexp(amax / 6.0)
        byte = np.where(mant > 0.5, ex, ex - 1) + 127
    byte = np.clip(np.where(amax > 0, byte, 1), 1, 254)
    scaled = (w * np.exp2(127.0 - byte)[:, None, :]).reshape(k, n).astype(np.float32)
    by_word = np.ascontiguousarray(scaled.reshape(k // 512, 128, 4, n).transpose(0, 1, 3, 2))
    if fmt == "e4m3":
        words = by_word.astype(ml_dtypes.float8_e4m3fn).view(np.uint8)
    else:
        c = by_word.astype(ml_dtypes.float4_e2m1fn).view(np.uint8) & 0xF
        words = (c[..., 0::2] | (c[..., 1::2] << 4)).reshape(k // 512, 128, 2 * n)
    return np.ascontiguousarray(words), np.ascontiguousarray(byte.astype(np.uint8).reshape(k // 512, 16, n))


def unpack_weight(words, scales, fmt):
    g, _, n = scales.shape
    words = np.ascontiguousarray(words).reshape(g, 128, n, -1)
    if fmt == "e4m3":
        vals = words.view(ml_dtypes.float8_e4m3fn).astype(np.float64)
    else:
        nib = np.empty((g, 128, n, 4), np.uint8)
        nib[..., 0::2] = words & 0xF
        nib[..., 1::2] = words >> 4
        vals = E2M1[nib]
    vals = vals * np.repeat(np.exp2(scales.astype(np.float64) - 127.0), 8, axis=1)[..., None]
    return vals.transpose(0, 1, 3, 2).reshape(g * 512, n)


def gelu(v):
    return 0.5 * v * (1.0 + np.tanh(np.sqrt(2.0 / np.pi) * (v + 0.044715 * v**3)))


def bf(x):
    return np.asarray(x, np.float32).astype(ml_dtypes.bfloat16)


def planes(Y):
    n, m = Y.shape
    b = f64(bf(Y)).reshape(n // 32, 32, m)
    amax = np.abs(b).max(1)
    byte = np.clip(np.where(amax > 0, np.frexp(amax)[1] - 1 + 127 - 7, 1), 1, 254)
    codes = (b * np.exp2(127.0 - byte)[:, None, :]).reshape(n, m).astype(np.float32).astype(ml_dtypes.float8_e4m3fn).view(np.uint8)
    words = codes.reshape(n // 512, 128, 4, m).transpose(0, 1, 3, 2)
    return np.ascontiguousarray(words), np.ascontiguousarray(byte.astype(np.uint8).reshape(n // 512, 16, m))


K, H, N, T, S, P = 1024, 512, 1024, 4096, 1024, 512

def setup_inputs():
    n = np.random.standard_normal
    s = mx_kscale(K)[:, None]
    u = mx_kscale(H)[:, None]
    rs = np.exp(0.8 * n(N))
    d = {}
    d["tab_words"], d["tab_scales"] = pack_weight(n((K, T)) * s, "e4m3")
    d["offs"] = striped(np.random.permutation(T)[:S])
    d["w1"] = (0.8 * n((K, H)) / K ** 0.5 / s).astype(np.float32)
    d["w2_words"], d["w2_scales"] = pack_weight(2.0 * n((K, H)) / K ** 0.5 / s, "e2m1")
    d["gain"] = (np.exp(0.3 * n(H)) * u[:, 0]).astype(np.float32)
    d["w3_words"], d["w3_scales"] = pack_weight(n((H, N)) / H ** 0.5 / u * rs, "e4m3")
    d["bench"] = (0.8 * n((N, S)) * rs[:, None]).astype(np.float32)
    d["pos1"] = striped(np.random.permutation(S)[:P])
    d["pos2"] = striped(np.random.permutation(S)[:P])
    return d

def reference(tab_words, tab_scales, offs, w1, w2_words, w2_scales, gain,
              w3_words, w3_scales, bench, pos1, pos2):
    v = unpack_weight(tab_words, tab_scales, "e4m3")[:, unstriped(offs)]
    w2 = unpack_weight(w2_words, w2_scales, "e2m1")
    w3 = unpack_weight(w3_words, w3_scales, "e4m3")
    lin = mxq(f64(w1), 0, "e4m3").T @ v
    bend = np.tanh(w2.T @ v)
    h = (lin + bend) * f64(gain)[:, None]
    g2 = (w3.T @ mxq(h, 0, "e4m3")) + f64(bench)
    push = np.abs(g2[:, unstriped(pos1)])
    draw = np.abs(g2[:, unstriped(pos2)])
    y = np.maximum(push, draw)
    words, scales = planes(y)
    return y, words, scales

@@ -1,0 +1,260 @@
+from contextlib import ExitStack
+
+import concourse.mybir as mybir
+
+K, H, N, T, S, M = 1024, 512, 1024, 4096, 1024, 512
+FLOPS = 2 * (2 * K * H * S + H * N * S)
+
+F32 = mybir.dt.float32
+BF16 = mybir.dt.bfloat16
+I32 = mybir.dt.int32
+U32 = mybir.dt.uint32
+U16 = mybir.dt.uint16
+U8 = mybir.dt.uint8
+FP8X4 = mybir.dt.float8_e4m3fn_x4
+FP4X4 = mybir.dt.float4_e2m1fn_x4
+ALU = mybir.AluOpType
+ACT = mybir.ActivationFunctionType
+
+P = 128
+PACK = 4
+BANK = 512
+QUADS = 4
+
+
+def tile_list_reed_pair_card_kernel(
+    tc, tab_words, tab_scales, offs, w1, w2_words, w2_scales, gain,
+    w3_words, w3_scales, bench, pos1, pos2, out_0, out_1, out_2,
+):
+    nc = tc.nc
+    passes = K // (P * PACK)
+    halves = S // BANK
+    groups = N // (P * PACK)
+
+    with ExitStack() as ctx:
+        keep = ctx.enter_context(tc.tile_pool(name="keep", bufs=1))
+        ring = ctx.enter_context(tc.tile_pool(name="ring", bufs=3))
+        psum = ctx.enter_context(tc.psum_pool(name="psum", bufs=8))
+
+        def held(shape, dtype, name, tag=None):
+            return keep.tile(shape, dtype, name=name, tag=tag or name, align_bytes=64)
+
+        offs_t = held([P, S // 16], U16, "offs_t")
+        pos1_t = held([P, M // 16], U16, "pos1_t")
+        pos2_t = held([P, M // 16], U16, "pos2_t")
+        nc.sync.dma_start(offs_t[:], offs)
+        nc.sync.dma_start(pos1_t[:], pos1)
+        nc.sync.dma_start(pos2_t[:], pos2)
+
+        gain_t = held([P, PACK], F32, "gain_t")
+        nc.sync.dma_start(gain_t[:], gain.rearrange("(p t) -> p t", t=PACK))
+        w2_raw = held([P, passes * H // 2], I32, "w2_raw", tag="w_raw")
+        nc.sync.dma_start(
+            w2_raw[:].rearrange("p (a c) -> p a c", a=passes),
+            w2_words.bitcast(I32).rearrange("a p c -> p a c"),
+        )
+
+        tab_sc = held([P, passes * T], U8, "tab_sc")
+        nc.vector.memset(tab_sc[:].bitcast(I32), 0)
+        for q in range(QUADS):
+            nc.scalar.dma_start(
+                tab_sc[32 * q : 32 * q + 4, :].bitcast(I32).rearrange("r (a c) -> r a c", a=passes),
+                tab_scales[:, 4 * q : 4 * q + 4, :].bitcast(I32).rearrange("a r c -> r a c"),
+            )
+
+        w2_sc_raw = held([P, passes * H], U8, "w2_sc_raw")
+        w3_sc_raw = held([P, N], U8, "w3_sc_raw")
+        nc.gpsimd.memset(w2_sc_raw[:].bitcast(I32), 0)
+        for q in range(QUADS):
+            nc.gpsimd.dma_start(
+                w2_sc_raw[32 * q : 32 * q + 4, :].bitcast(I32).rearrange("r (a c) -> r a c", a=passes),
+                w2_scales[:, 4 * q : 4 * q + 4, :].bitcast(I32).rearrange("a r c -> r a c"),
+            )
+        nc.gpsimd.memset(w3_sc_raw[:].bitcast(I32), 0)
+        for q in range(QUADS):
+            nc.gpsimd.dma_start(
+                w3_sc_raw[32 * q : 32 * q + 4, :].bitcast(I32),
+                w3_scales[0, 4 * q : 4 * q + 4, :].bitcast(I32),
+            )
+
+        tab_w = [held([P, T], I32, f"tab_w{a}", tag=f"big{a}") for a in range(passes)]
+        for a in range(passes):
+            nc.sync.dma_start(tab_w[a][:], tab_words[a].rearrange("p n i -> p (n i)").bitcast(I32))
+        w1_raw = [held([P, PACK, H], F32, f"w1_raw{a}") for a in range(passes)]
+        for a in range(passes):
+            nc.sync.dma_start(
+                w1_raw[a][:], w1[a * 512 : (a + 1) * 512, :].rearrange("(p i) c -> p i c", i=PACK)
+            )
+
+        warm = held([P, PACK], F32, "warm")
+        nc.scalar.activation(warm[:], gain_t[:], ACT.Tanh)
+
+        w2_c = held([P, passes * H], U16, "w2_c")
+        nc.vector.tensor_copy(
+            w2_c[:].rearrange("p (a t q) -> p a q t", a=passes, t=PACK),
+            w2_raw[:].bitcast(U16).rearrange("p (a q t) -> p a q t", a=passes, t=PACK),
+        )
+        v_sc = [held([P, S], U8, f"v_sc{a}") for a in range(passes)]
+        v_c = [[held([P, BANK], U32, f"v_c{a}{j}") for j in range(halves)] for a in range(passes)]
+        w2_sc = held([P, passes * H], U8, "w2_sc")
+        cols16 = BANK // 16
+        for a in range(passes):
+            nc.vector.tensor_copy(v_sc[a][:], tab_sc[:, a * T : (a + 1) * T].indirect(offs_t[:]))
+            if a == 0:
+                nc.vector.tensor_copy(
+                    w2_sc[:].rearrange("p (a t q) -> p a q t", a=passes, t=PACK),
+                    w2_sc_raw[:].rearrange("p (a q t) -> p a q t", a=passes, t=PACK),
+                )
+            for j in range(halves):
+                nc.vector.tensor_copy(
+                    v_c[a][j][:],
+                    tab_w[a][:].bitcast(U32).indirect(offs_t[:, j * cols16 : (j + 1) * cols16]),
+                )
+
+        w3_raw = held([P, N], I32, "w3_raw", tag="w_raw")
+        nc.sync.dma_start(w3_raw[:], w3_words[0].rearrange("p n i -> p (n i)").bitcast(I32))
+        bench_t = [held([P, PACK, S], F32, f"bench{g}", tag=f"big{g}") for g in range(groups)]
+        for g in range(groups):
+            nc.sync.dma_start(
+                bench_t[g][:], bench[g * 512 : (g + 1) * 512, :].rearrange("(p t) j -> p t j", t=PACK)
+            )
+
+        units = [(j, t) for j in range(halves) for t in range(PACK)]
+        bend = {u: psum.tile([P, BANK], F32, name="acc") for u in units}
+        w2_bytes = w2_c[:].bitcast(U8)
+        for a in range(passes):
+            for j, t in units:
+                c0 = a * H + t * P
+                nc.tensor.matmul_mx(
+                    out=bend[j, t][:],
+                    lhsT=w2_bytes[:, 2 * c0 : 2 * (c0 + P)].bitcast(FP4X4),
+                    lhsT_scale=w2_sc[:, c0 : c0 + P],
+                    rhs=v_c[a][j][:].bitcast(FP8X4),
+                    rhs_scale=v_sc[a][:, j * BANK : (j + 1) * BANK],
+                    start=(a == 0),
+                    stop=(a == passes - 1),
+                )
+        bent = {u: held([P, BANK], F32, f"bent{u[0]}{u[1]}") for u in units}
+        for j in range(halves):
+            for t in range(PACK):
+                nc.scalar.activation(bent[j, t][:], bend[j, t][:], ACT.Tanh)
+            for t in range(PACK):
+                nc.scalar.activation(bent[j, t][:], bent[j, t][:], ACT.Copy, scale=gain_t[:, t : t + 1])
+
+        w1_c = [held([P, H], U32, f"w1_c{a}") for a in range(passes)]
+        w1_sc = [held([P, H], U8, f"w1_sc{a}") for a in range(passes)]
+        w1_b = [held([P, PACK * H], BF16, f"w1_b{a}") for a in range(passes)]
+        for a in range(passes):
+            nc.vector.tensor_copy(
+                w1_b[a][:].rearrange("p (t q i) -> p q i t", t=PACK, i=PACK),
+                w1_raw[a][:].rearrange("p i (q t) -> p q i t", t=PACK),
+            )
+            nc.vector.quantize_mx(out=w1_c[a][:].bitcast(FP8X4), scales=w1_sc[a][:], in_=w1_b[a][:])
+
+        lin = {u: psum.tile([P, BANK], F32, name="acc") for u in units}
+        for a in range(passes):
+            for j, t in units:
+                nc.tensor.matmul_mx(
+                    out=lin[j, t][:],
+                    lhsT=w1_c[a][:, t * P : (t + 1) * P].bitcast(FP8X4),
+                    lhsT_scale=w1_sc[a][:, t * P : (t + 1) * P],
+                    rhs=v_c[a][j][:].bitcast(FP8X4),
+                    rhs_scale=v_sc[a][:, j * BANK : (j + 1) * BANK],
+                    start=(a == 0),
+                    stop=(a == passes - 1),
+                )
+
+        w3_c = held([P, N], I32, "w3_c")
+        nc.vector.tensor_copy(
+            w3_c[:].rearrange("p (g t q) -> p g q t", g=groups, t=PACK),
+            w3_raw[:].rearrange("p (g q t) -> p g q t", g=groups, t=PACK),
+        )
+
+        w3_sc = held([P, N], U8, "w3_sc")
+        nc.vector.tensor_copy(
+            w3_sc[:].rearrange("p (g t q) -> p g q t", g=groups, t=PACK),
+            w3_sc_raw[:].rearrange("p (g q t) -> p g q t", g=groups, t=PACK),
+        )
+
+        h_rows = [held([P, PACK, BANK], BF16, f"h_rows{j}") for j in range(halves)]
+        h_b = [held([P, PACK * BANK], BF16, f"h_b{j}") for j in range(halves)]
+        h_c = [held([P, BANK], U32, f"h_c{j}") for j in range(halves)]
+        h_sc = [held([P, BANK], U8, f"h_sc{j}") for j in range(halves)]
+        weave = [nc.vector.tensor_copy, nc.scalar.copy]
+        for j in range(halves):
+            for t in range(PACK):
+                nc.vector.scalar_tensor_tensor(
+                    h_rows[j][:, t, :], lin[j, t][:], gain_t[:, t : t + 1], bent[j, t][:], ALU.mult, ALU.add
+                )
+            weave[j](
+                h_b[j][:].rearrange("p (c i t) -> p c t i", i=4, t=PACK),
+                h_rows[j][:].rearrange("p t (c i) -> p c t i", i=4),
+            )
+            nc.vector.quantize_mx(out=h_c[j][:].bitcast(FP8X4), scales=h_sc[j][:], in_=h_b[j][:])
+
+        slices = [(g, t) for g in range(groups) for t in range(PACK)]
+        g2 = {s: held([P, S], F32, f"g2_{s[0]}{s[1]}") for s in slices}
+
+        def second(j, g, t):
+            c0 = (g * PACK + t) * P
+            acc = psum.tile([P, BANK], F32, name="acc")
+            nc.tensor.matmul_mx(
+                out=acc[:],
+                lhsT=w3_c[:, c0 : c0 + P].bitcast(FP8X4),
+                lhsT_scale=w3_sc[:, c0 : c0 + P],
+                rhs=h_c[j][:].bitcast(FP8X4),
+                rhs_scale=h_sc[j][:],
+                start=True,
+                stop=True,
+            )
+            cols = slice(j * BANK, (j + 1) * BANK)
+            nc.vector.tensor_tensor(g2[g, t][:, cols], acc[:], bench_t[g][:, t, cols], ALU.add)
+
+        y = [held([P, PACK, M], F32, f"y{g}") for g in range(groups)]
+        y_b = [held([P, PACK * M], BF16, f"y_b{g}") for g in range(groups)]
+        y_c = [held([P, M], I32, f"y_c{g}") for g in range(groups)]
+        y_sc = held([P, groups * M], U8, "y_sc")
+        pair = {}
+
+        def pick(g, t):
+            both = ring.tile([P, 2 * M], F32, name="both")
+            nc.vector.tensor_copy(both[:, 0:M], g2[g, t][:].indirect(pos1_t[:]))
+            nc.vector.tensor_copy(both[:, M : 2 * M], g2[g, t][:].indirect(pos2_t[:]))
+            nc.scalar.activation(both[:], both[:], ACT.Abs)
+            pair[g, t] = both
+
+        def larger(g, t):
+            both = pair[g, t]
+            nc.vector.tensor_tensor(y[g][:, t, :], both[:, 0:M], both[:, M : 2 * M], ALU.max)
+            rows = out_0[g * 512 : (g + 1) * 512, :].rearrange("(p t) m -> p t m", t=PACK)
+            nc.sync.dma_start(rows[:, t, :], y[g][:, t, :])
+            if t == PACK - 1:
+                nc.scalar.copy(
+                    y_b[g][:].rearrange("p (c i t) -> p c t i", i=4, t=PACK),
+                    y[g][:].rearrange("p t (c i) -> p c t i", i=4),
+                )
+
+        def planes(g):
+            nc.vector.quantize_mx(
+                out=y_c[g][:].bitcast(FP8X4), scales=y_sc[:, g * M : (g + 1) * M], in_=y_b[g][:]
+            )
+            nc.sync.dma_start(out_1[g].rearrange("p m t -> p (m t)").bitcast(I32), y_c[g][:])
+
+        for g, t in slices:
+            second(0, g, t)
+        second(1, *slices[0])
+        for n, s in enumerate(slices):
+            if n + 1 < len(slices):
+                second(1, *slices[n + 1])
+            pick(*s)
+            if n > 0:
+                larger(*slices[n - 1])
+            if n == PACK + 1:
+                planes(0)
+        larger(*slices[-1])
+        planes(groups - 1)
+        for q in range(QUADS):
+            nc.scalar.dma_start(
+                out_2[:, 4 * q : 4 * q + 4, :].bitcast(I32).rearrange("g r m -> r g m"),
+                y_sc[32 * q : 32 * q + 4, :].bitcast(I32).rearrange("r (g m) -> r g m", g=groups),
+            )

@@ -42,48 +42,48 @@ def tile_list_reed_pair_card_kernel(
         offs_t = held([P, S // 16], U16, "offs_t")
         pos1_t = held([P, M // 16], U16, "pos1_t")
         pos2_t = held([P, M // 16], U16, "pos2_t")
-        nc.sync.dma_start(offs_t[:], offs)
-        nc.sync.dma_start(pos1_t[:], pos1)
-        nc.sync.dma_start(pos2_t[:], pos2)
+        tab_sc = held([P, passes * T], U8, "tab_sc")
+        w2_sc_raw = held([P, passes * H], U8, "w2_sc_raw")
+        w3_sc_raw = held([P, N], U8, "w3_sc_raw")
+        nc.vector.memset(tab_sc[:, 0 : 5 * T // 4].bitcast(I32), 0)
+        nc.gpsimd.memset(tab_sc[:, 5 * T // 4 : 2 * T].bitcast(I32), 0)
+        nc.vector.memset(w2_sc_raw[:].bitcast(I32), 0)
+        nc.gpsimd.memset(w3_sc_raw[:].bitcast(I32), 0)
 
-        gain_t = held([P, PACK], F32, "gain_t")
-        nc.sync.dma_start(gain_t[:], gain.rearrange("(p t) -> p t", t=PACK))
-        w2_raw = held([P, passes * H // 2], I32, "w2_raw", tag="w_raw")
+        nc.sync.dma_start(offs_t[:], offs)
+        w2_raw = held([P, passes * H // 2], I32, "w2_raw")
         nc.sync.dma_start(
             w2_raw[:].rearrange("p (a c) -> p a c", a=passes),
             w2_words.bitcast(I32).rearrange("a p c -> p a c"),
         )
-
-        tab_sc = held([P, passes * T], U8, "tab_sc")
-        nc.vector.memset(tab_sc[:].bitcast(I32), 0)
+        gain_t = held([P, PACK], F32, "gain_t")
+        nc.sync.dma_start(gain_t[:], gain.rearrange("(p t) -> p t", t=PACK))
         for q in range(QUADS):
-            nc.scalar.dma_start(
+            nc.sync.dma_start(
                 tab_sc[32 * q : 32 * q + 4, :].bitcast(I32).rearrange("r (a c) -> r a c", a=passes),
                 tab_scales[:, 4 * q : 4 * q + 4, :].bitcast(I32).rearrange("a r c -> r a c"),
             )
-
-        w2_sc_raw = held([P, passes * H], U8, "w2_sc_raw")
-        w3_sc_raw = held([P, N], U8, "w3_sc_raw")
-        nc.gpsimd.memset(w2_sc_raw[:].bitcast(I32), 0)
+        tab_w = [held([P, T], I32, f"tab_w{a}", tag=f"big{a}") for a in range(passes)]
+        nc.sync.dma_start(tab_w[0][:], tab_words[0].rearrange("p n i -> p (n i)").bitcast(I32))
         for q in range(QUADS):
-            nc.gpsimd.dma_start(
+            nc.sync.dma_start(
                 w2_sc_raw[32 * q : 32 * q + 4, :].bitcast(I32).rearrange("r (a c) -> r a c", a=passes),
                 w2_scales[:, 4 * q : 4 * q + 4, :].bitcast(I32).rearrange("a r c -> r a c"),
             )
-        nc.gpsimd.memset(w3_sc_raw[:].bitcast(I32), 0)
-        for q in range(QUADS):
-            nc.gpsimd.dma_start(
-                w3_sc_raw[32 * q : 32 * q + 4, :].bitcast(I32),
-                w3_scales[0, 4 * q : 4 * q + 4, :].bitcast(I32),
-            )
-
-        tab_w = [held([P, T], I32, f"tab_w{a}", tag=f"big{a}") for a in range(passes)]
-        for a in range(passes):
-            nc.sync.dma_start(tab_w[a][:], tab_words[a].rearrange("p n i -> p (n i)").bitcast(I32))
+        nc.sync.dma_start(tab_w[1][:], tab_words[1].rearrange("p n i -> p (n i)").bitcast(I32))
         w1_raw = [held([P, PACK, H], F32, f"w1_raw{a}") for a in range(passes)]
         for a in range(passes):
             nc.sync.dma_start(
                 w1_raw[a][:], w1[a * 512 : (a + 1) * 512, :].rearrange("(p i) c -> p i c", i=PACK)
+            )
+        nc.sync.dma_start(pos1_t[:], pos1)
+        nc.sync.dma_start(pos2_t[:], pos2)
+        w3_raw = held([P, N], I32, "w3_raw")
+        nc.sync.dma_start(w3_raw[:], w3_words[0].rearrange("p n i -> p (n i)").bitcast(I32))
+        for q in range(QUADS):
+            nc.sync.dma_start(
+                w3_sc_raw[32 * q : 32 * q + 4, :].bitcast(I32),
+                w3_scales[0, 4 * q : 4 * q + 4, :].bitcast(I32),
             )
 
         warm = held([P, PACK], F32, "warm")
@@ -100,19 +100,19 @@ def tile_list_reed_pair_card_kernel(
         cols16 = BANK // 16
         for a in range(passes):
             nc.vector.tensor_copy(v_sc[a][:], tab_sc[:, a * T : (a + 1) * T].indirect(offs_t[:]))
-            if a == 0:
-                nc.vector.tensor_copy(
-                    w2_sc[:].rearrange("p (a t q) -> p a q t", a=passes, t=PACK),
-                    w2_sc_raw[:].rearrange("p (a q t) -> p a q t", a=passes, t=PACK),
-                )
+        for a in range(passes):
             for j in range(halves):
                 nc.vector.tensor_copy(
                     v_c[a][j][:],
                     tab_w[a][:].bitcast(U32).indirect(offs_t[:, j * cols16 : (j + 1) * cols16]),
                 )
+                if a == 0:
+                    cols = slice(j * H, (j + 1) * H)
+                    nc.vector.tensor_copy(
+                        w2_sc[:, cols].rearrange("p (t q) -> p q t", t=PACK),
+                        w2_sc_raw[:, cols].rearrange("p (q t) -> p q t", t=PACK),
+                    )
 
-        w3_raw = held([P, N], I32, "w3_raw", tag="w_raw")
-        nc.sync.dma_start(w3_raw[:], w3_words[0].rearrange("p n i -> p (n i)").bitcast(I32))
         bench_t = [held([P, PACK, S], F32, f"bench{g}", tag=f"big{g}") for g in range(groups)]
         for g in range(groups):
             nc.sync.dma_start(
@@ -120,10 +120,11 @@ def tile_list_reed_pair_card_kernel(
             )
 
         units = [(j, t) for j in range(halves) for t in range(PACK)]
+        ordered = [(j, a, t) for j in range(halves) for a in range(passes) for t in range(PACK)]
         bend = {u: psum.tile([P, BANK], F32, name="acc") for u in units}
         w2_bytes = w2_c[:].bitcast(U8)
-        for a in range(passes):
-            for j, t in units:
+        for j, a, t in ordered:
+            if True:
                 c0 = a * H + t * P
                 nc.tensor.matmul_mx(
                     out=bend[j, t][:],
@@ -152,8 +153,8 @@ def tile_list_reed_pair_card_kernel(
             nc.vector.quantize_mx(out=w1_c[a][:].bitcast(FP8X4), scales=w1_sc[a][:], in_=w1_b[a][:])
 
         lin = {u: psum.tile([P, BANK], F32, name="acc") for u in units}
-        for a in range(passes):
-            for j, t in units:
+        for j, a, t in ordered:
+            if True:
                 nc.tensor.matmul_mx(
                     out=lin[j, t][:],
                     lhsT=w1_c[a][:, t * P : (t + 1) * P].bitcast(FP8X4),
@@ -164,6 +165,10 @@ def tile_list_reed_pair_card_kernel(
                     stop=(a == passes - 1),
                 )
 
+        h_rows = [held([P, PACK, BANK], BF16, f"h_rows{j}") for j in range(halves)]
+        h_b = [held([P, PACK * BANK], BF16, f"h_b{j}") for j in range(halves)]
+        h_c = [held([P, BANK], U32, f"h_c{j}") for j in range(halves)]
+        h_sc = [held([P, BANK], U8, f"h_sc{j}") for j in range(halves)]
         w3_c = held([P, N], I32, "w3_c")
         nc.vector.tensor_copy(
             w3_c[:].rearrange("p (g t q) -> p g q t", g=groups, t=PACK),
@@ -176,17 +181,12 @@ def tile_list_reed_pair_card_kernel(
             w3_sc_raw[:].rearrange("p (g q t) -> p g q t", g=groups, t=PACK),
         )
 
-        h_rows = [held([P, PACK, BANK], BF16, f"h_rows{j}") for j in range(halves)]
-        h_b = [held([P, PACK * BANK], BF16, f"h_b{j}") for j in range(halves)]
-        h_c = [held([P, BANK], U32, f"h_c{j}") for j in range(halves)]
-        h_sc = [held([P, BANK], U8, f"h_sc{j}") for j in range(halves)]
-        weave = [nc.vector.tensor_copy, nc.scalar.copy]
-        for j in range(halves):
+        for j, copy in enumerate((nc.vector.tensor_copy, nc.scalar.copy)):
             for t in range(PACK):
                 nc.vector.scalar_tensor_tensor(
                     h_rows[j][:, t, :], lin[j, t][:], gain_t[:, t : t + 1], bent[j, t][:], ALU.mult, ALU.add
                 )
-            weave[j](
+            copy(
                 h_b[j][:].rearrange("p (c i t) -> p c t i", i=4, t=PACK),
                 h_rows[j][:].rearrange("p t (c i) -> p c t i", i=4),
             )
@@ -216,43 +216,59 @@ def tile_list_reed_pair_card_kernel(
         y_sc = held([P, groups * M], U8, "y_sc")
         pair = {}
 
-        def pick(g, t):
+        def pick(g, t, m0, m1):
+            width = m1 - m0
             both = ring.tile([P, 2 * M], F32, name="both")
-            nc.vector.tensor_copy(both[:, 0:M], g2[g, t][:].indirect(pos1_t[:]))
-            nc.vector.tensor_copy(both[:, M : 2 * M], g2[g, t][:].indirect(pos2_t[:]))
-            nc.scalar.activation(both[:], both[:], ACT.Abs)
-            pair[g, t] = both
-
-        def larger(g, t):
-            both = pair[g, t]
-            nc.vector.tensor_tensor(y[g][:, t, :], both[:, 0:M], both[:, M : 2 * M], ALU.max)
-            rows = out_0[g * 512 : (g + 1) * 512, :].rearrange("(p t) m -> p t m", t=PACK)
-            nc.sync.dma_start(rows[:, t, :], y[g][:, t, :])
-            if t == PACK - 1:
-                nc.scalar.copy(
-                    y_b[g][:].rearrange("p (c i t) -> p c t i", i=4, t=PACK),
-                    y[g][:].rearrange("p t (c i) -> p c t i", i=4),
+            for n, pos_t in enumerate((pos1_t, pos2_t)):
+                nc.vector.tensor_copy(
+                    both[:, n * width : (n + 1) * width], g2[g, t][:].indirect(pos_t[:, m0 // 16 : m1 // 16])
                 )
+            nc.scalar.activation(both[:, 0 : 2 * width], both[:, 0 : 2 * width], ACT.Abs)
+            pair[g, t, m0] = both
 
-        def planes(g):
-            nc.vector.quantize_mx(
-                out=y_c[g][:].bitcast(FP8X4), scales=y_sc[:, g * M : (g + 1) * M], in_=y_b[g][:]
+        def larger(g, t, m0, m1):
+            width = m1 - m0
+            both = pair[g, t, m0]
+            nc.vector.tensor_tensor(y[g][:, t, m0:m1], both[:, 0:width], both[:, width : 2 * width], ALU.max)
+            rows = out_0[g * 512 : (g + 1) * 512, :].rearrange("(p t) m -> p t m", t=PACK)
+            nc.sync.dma_start(rows[:, t, m0:m1], y[g][:, t, m0:m1])
+
+        def weave(copy, g, m0, m1):
+            copy(
+                y_b[g][:, PACK * m0 : PACK * m1].rearrange("p (c i t) -> p c t i", i=4, t=PACK),
+                y[g][:, :, m0:m1].rearrange("p t (c i) -> p c t i", i=4),
             )
-            nc.sync.dma_start(out_1[g].rearrange("p m t -> p (m t)").bitcast(I32), y_c[g][:])
 
+        def planes(g, m0, m1):
+            nc.vector.quantize_mx(
+                out=y_c[g][:, m0:m1].bitcast(FP8X4),
+                scales=y_sc[:, g * M + m0 : g * M + m1],
+                in_=y_b[g][:, PACK * m0 : PACK * m1],
+            )
+            nc.sync.dma_start(
+                out_1[g].rearrange("p m t -> p (m t)").bitcast(I32)[:, m0:m1], y_c[g][:, m0:m1]
+            )
+
+        steps = [(g, t, 0, M) for g, t in slices[:-1]]
+        steps.extend([slices[-1] + (0, M // 2), slices[-1] + (M // 2, M)])
         for g, t in slices:
             second(0, g, t)
         second(1, *slices[0])
-        for n, s in enumerate(slices):
+        for n, s in enumerate(steps):
             if n + 1 < len(slices):
                 second(1, *slices[n + 1])
             pick(*s)
             if n > 0:
-                larger(*slices[n - 1])
-            if n == PACK + 1:
-                planes(0)
-        larger(*slices[-1])
-        planes(groups - 1)
+                larger(*steps[n - 1])
+            if n == PACK:
+                weave(nc.scalar.copy, 0, 0, M)
+            if n == PACK + 2:
+                planes(0, 0, M)
+        weave(nc.scalar.copy, 1, 0, M // 2)
+        larger(*steps[-1])
+        weave(nc.vector.tensor_copy, 1, M // 2, M)
+        planes(1, 0, M // 2)
+        planes(1, M // 2, M)
         for q in range(QUADS):
             nc.scalar.dma_start(
                 out_2[:, 4 * q : 4 * q + 4, :].bitcast(I32).rearrange("g r m -> r g m"),

@@ -1,6 +1,7 @@
 from contextlib import ExitStack
 
 import concourse.mybir as mybir
+from concourse.masks import make_identity
 
 K, H, N, T, S, M = 1024, 512, 1024, 4096, 1024, 512
 FLOPS = 2 * (2 * K * H * S + H * N * S)
@@ -34,21 +35,30 @@ def tile_list_reed_pair_card_kernel(
     with ExitStack() as ctx:
         keep = ctx.enter_context(tc.tile_pool(name="keep", bufs=1))
         ring = ctx.enter_context(tc.tile_pool(name="ring", bufs=3))
-        psum = ctx.enter_context(tc.psum_pool(name="psum", bufs=8))
+        overlay = ctx.enter_context(tc.tile_pool(name="overlay", bufs=1))
+        psum = ctx.enter_context(tc.psum_pool(name="psum", bufs=1))
 
         def held(shape, dtype, name, tag=None):
             return keep.tile(shape, dtype, name=name, tag=tag or name, align_bytes=64)
 
+        def laid(shape, dtype, name, kib):
+            return overlay.tile(shape, dtype, name=name, align_bytes=64, offset=kib * 1024)
+
+        def bank(b):
+            return psum.tile([P, BANK], F32, name=f"bank{b}")
+
         offs_t = held([P, S // 16], U16, "offs_t")
         pos1_t = held([P, M // 16], U16, "pos1_t")
         pos2_t = held([P, M // 16], U16, "pos2_t")
-        tab_sc = held([P, passes * T], U8, "tab_sc")
+        tab_sc = laid([P, T], U8, "tab_sc", 7)
         w2_sc_raw = held([P, passes * H], U8, "w2_sc_raw")
-        w3_sc_raw = held([P, N], U8, "w3_sc_raw")
-        nc.vector.memset(tab_sc[:, 0 : 5 * T // 4].bitcast(I32), 0)
-        nc.gpsimd.memset(tab_sc[:, 5 * T // 4 : 2 * T].bitcast(I32), 0)
+        v_sc1 = held([P, S], U8, "v_sc1")
+        nc.vector.memset(tab_sc[:, 0 : T // 2].bitcast(I32), 0)
+        nc.gpsimd.memset(tab_sc[:, T // 2 : T].bitcast(I32), 0)
         nc.vector.memset(w2_sc_raw[:].bitcast(I32), 0)
-        nc.gpsimd.memset(w3_sc_raw[:].bitcast(I32), 0)
+        nc.gpsimd.memset(v_sc1[:].bitcast(I32), 0)
+        ident = held([P, P], F32, "ident")
+        make_identity(nc, ident[:])
 
         nc.sync.dma_start(offs_t[:], offs)
         w2_raw = held([P, passes * H // 2], I32, "w2_raw")
@@ -60,31 +70,19 @@ def tile_list_reed_pair_card_kernel(
         nc.sync.dma_start(gain_t[:], gain.rearrange("(p t) -> p t", t=PACK))
         for q in range(QUADS):
             nc.sync.dma_start(
-                tab_sc[32 * q : 32 * q + 4, :].bitcast(I32).rearrange("r (a c) -> r a c", a=passes),
-                tab_scales[:, 4 * q : 4 * q + 4, :].bitcast(I32).rearrange("a r c -> r a c"),
+                tab_sc[32 * q : 32 * q + 4 * passes, :].bitcast(I32),
+                tab_scales[:, 4 * q : 4 * q + 4, :].bitcast(I32),
             )
-        tab_w = [held([P, T], I32, f"tab_w{a}", tag=f"big{a}") for a in range(passes)]
+        tab_w = [laid([P, T], I32, f"tab_w{a}", 17 + 16 * a) for a in range(passes)]
         nc.sync.dma_start(tab_w[0][:], tab_words[0].rearrange("p n i -> p (n i)").bitcast(I32))
         for q in range(QUADS):
             nc.sync.dma_start(
-                w2_sc_raw[32 * q : 32 * q + 4, :].bitcast(I32).rearrange("r (a c) -> r a c", a=passes),
-                w2_scales[:, 4 * q : 4 * q + 4, :].bitcast(I32).rearrange("a r c -> r a c"),
+                w2_sc_raw[q:P:32, :].bitcast(I32).rearrange("r (a c) -> r a c", a=passes),
+                w2_scales[:, q:16:4, :].bitcast(I32).rearrange("a r c -> r a c"),
             )
         nc.sync.dma_start(tab_w[1][:], tab_words[1].rearrange("p n i -> p (n i)").bitcast(I32))
-        w1_raw = [held([P, PACK, H], F32, f"w1_raw{a}") for a in range(passes)]
-        for a in range(passes):
-            nc.sync.dma_start(
-                w1_raw[a][:], w1[a * 512 : (a + 1) * 512, :].rearrange("(p i) c -> p i c", i=PACK)
-            )
         nc.sync.dma_start(pos1_t[:], pos1)
         nc.sync.dma_start(pos2_t[:], pos2)
-        w3_raw = held([P, N], I32, "w3_raw")
-        nc.sync.dma_start(w3_raw[:], w3_words[0].rearrange("p n i -> p (n i)").bitcast(I32))
-        for q in range(QUADS):
-            nc.sync.dma_start(
-                w3_sc_raw[32 * q : 32 * q + 4, :].bitcast(I32),
-                w3_scales[0, 4 * q : 4 * q + 4, :].bitcast(I32),
-            )
 
         warm = held([P, PACK], F32, "warm")
         nc.scalar.activation(warm[:], gain_t[:], ACT.Tanh)
@@ -94,12 +92,23 @@ def tile_list_reed_pair_card_kernel(
             w2_c[:].rearrange("p (a t q) -> p a q t", a=passes, t=PACK),
             w2_raw[:].bitcast(U16).rearrange("p (a q t) -> p a q t", a=passes, t=PACK),
         )
-        v_sc = [held([P, S], U8, f"v_sc{a}") for a in range(passes)]
         v_c = [[held([P, BANK], U32, f"v_c{a}{j}") for j in range(halves)] for a in range(passes)]
         w2_sc = held([P, passes * H], U8, "w2_sc")
         cols16 = BANK // 16
+        v_sc0 = held([P, S], U8, "v_sc0")
+        nc.vector.tensor_copy(v_sc0[:], tab_sc[:].indirect(offs_t[:]))
+        for q in range(QUADS):
+            nc.sync.dma_start(v_sc1[q:P:32, :].bitcast(I32), v_sc0[4 + q : P : 32, :].bitcast(I32))
+        v_sc = [v_sc0, v_sc1]
+        w1_raw = [laid([P, PACK, H], F32, f"w1_raw{a}", 9 * a) for a in range(passes)]
         for a in range(passes):
-            nc.vector.tensor_copy(v_sc[a][:], tab_sc[:, a * T : (a + 1) * T].indirect(offs_t[:]))
+            nc.sync.dma_start(
+                w1_raw[a][:], w1[a * 512 : (a + 1) * 512, :].rearrange("(p i) c -> p i c", i=PACK)
+            )
+        w3_sc_raw = laid([P, N], U8, "w3_sc_raw", 8)
+        nc.gpsimd.memset(w3_sc_raw[:].bitcast(I32), 0)
+        for q in range(QUADS):
+            nc.sync.dma_start(w3_sc_raw[q:P:32, :].bitcast(I32), w3_scales[0, q:16:4, :].bitcast(I32))
         for a in range(passes):
             for j in range(halves):
                 nc.vector.tensor_copy(
@@ -112,16 +121,18 @@ def tile_list_reed_pair_card_kernel(
                         w2_sc[:, cols].rearrange("p (t q) -> p q t", t=PACK),
                         w2_sc_raw[:, cols].rearrange("p (q t) -> p q t", t=PACK),
                     )
+        w3_raw = laid([P, N], I32, "w3_raw", 17)
+        nc.sync.dma_start(w3_raw[:], w3_words[0].rearrange("p n i -> p (n i)").bitcast(I32))
 
-        bench_t = [held([P, PACK, S], F32, f"bench{g}", tag=f"big{g}") for g in range(groups)]
-        for g in range(groups):
+        bench_t = [laid([P, PACK, S], F32, f"bench{g}", 37 - 16 * g) for g in range(groups)]
+        for g in reversed(range(groups)):
             nc.sync.dma_start(
                 bench_t[g][:], bench[g * 512 : (g + 1) * 512, :].rearrange("(p t) j -> p t j", t=PACK)
             )
 
         units = [(j, t) for j in range(halves) for t in range(PACK)]
         ordered = [(j, a, t) for j in range(halves) for a in range(passes) for t in range(PACK)]
-        bend = {u: psum.tile([P, BANK], F32, name="acc") for u in units}
+        bend = {u: bank(n) for n, u in enumerate(units)}
         w2_bytes = w2_c[:].bitcast(U8)
         for j, a, t in ordered:
             if True:
@@ -135,7 +146,7 @@ def tile_list_reed_pair_card_kernel(
                     start=(a == 0),
                     stop=(a == passes - 1),
                 )
-        bent = {u: held([P, BANK], F32, f"bent{u[0]}{u[1]}") for u in units}
+        bent = {u: held([P, BANK], F32, f"bent{n}", tag=f"small{n}") for n, u in enumerate(units)}
         for j in range(halves):
             for t in range(PACK):
                 nc.scalar.activation(bent[j, t][:], bend[j, t][:], ACT.Tanh)
@@ -152,33 +163,32 @@ def tile_list_reed_pair_card_kernel(
             )
             nc.vector.quantize_mx(out=w1_c[a][:].bitcast(FP8X4), scales=w1_sc[a][:], in_=w1_b[a][:])
 
-        lin = {u: psum.tile([P, BANK], F32, name="acc") for u in units}
-        for j, a, t in ordered:
-            if True:
+        lin = {u: bank(n) for n, u in enumerate(units)}
+        for j, n, t in ordered:
+            for a in [n if j == 0 else passes - 1 - n]:
                 nc.tensor.matmul_mx(
                     out=lin[j, t][:],
                     lhsT=w1_c[a][:, t * P : (t + 1) * P].bitcast(FP8X4),
                     lhsT_scale=w1_sc[a][:, t * P : (t + 1) * P],
                     rhs=v_c[a][j][:].bitcast(FP8X4),
                     rhs_scale=v_sc[a][:, j * BANK : (j + 1) * BANK],
-                    start=(a == 0),
-                    stop=(a == passes - 1),
+                    start=(n == 0),
+                    stop=(n == passes - 1),
                 )
 
         h_rows = [held([P, PACK, BANK], BF16, f"h_rows{j}") for j in range(halves)]
         h_b = [held([P, PACK * BANK], BF16, f"h_b{j}") for j in range(halves)]
         h_c = [held([P, BANK], U32, f"h_c{j}") for j in range(halves)]
         h_sc = [held([P, BANK], U8, f"h_sc{j}") for j in range(halves)]
-        w3_c = held([P, N], I32, "w3_c")
+        w3_c = held([P, BANK], I32, "w3_c")
         nc.vector.tensor_copy(
-            w3_c[:].rearrange("p (g t q) -> p g q t", g=groups, t=PACK),
-            w3_raw[:].rearrange("p (g q t) -> p g q t", g=groups, t=PACK),
+            w3_c[:].rearrange("p (t q) -> p q t", t=PACK),
+            w3_raw[:, 0:BANK].rearrange("p (q t) -> p q t", t=PACK),
         )
-
-        w3_sc = held([P, N], U8, "w3_sc")
+        w3_sc = held([P, BANK], U8, "w3_sc")
         nc.vector.tensor_copy(
-            w3_sc[:].rearrange("p (g t q) -> p g q t", g=groups, t=PACK),
-            w3_sc_raw[:].rearrange("p (g q t) -> p g q t", g=groups, t=PACK),
+            w3_sc[:].rearrange("p (t q) -> p q t", t=PACK),
+            w3_sc_raw[:, 0:BANK].rearrange("p (q t) -> p q t", t=PACK),
         )
 
         for j, copy in enumerate((nc.vector.tensor_copy, nc.scalar.copy)):
@@ -194,10 +204,9 @@ def tile_list_reed_pair_card_kernel(
 
         slices = [(g, t) for g in range(groups) for t in range(PACK)]
         g2 = {s: held([P, S], F32, f"g2_{s[0]}{s[1]}") for s in slices}
-
-        def second(j, g, t):
-            c0 = (g * PACK + t) * P
-            acc = psum.tile([P, BANK], F32, name="acc")
+        def direct(j, t):
+            c0 = t * P
+            acc = bank(j * PACK + t)
             nc.tensor.matmul_mx(
                 out=acc[:],
                 lhsT=w3_c[:, c0 : c0 + P].bitcast(FP8X4),
@@ -208,10 +217,55 @@ def tile_list_reed_pair_card_kernel(
                 stop=True,
             )
             cols = slice(j * BANK, (j + 1) * BANK)
-            nc.vector.tensor_tensor(g2[g, t][:, cols], acc[:], bench_t[g][:, t, cols], ALU.add)
+            nc.vector.tensor_tensor(g2[0, t][:, cols], acc[:], bench_t[0][:, t, cols], ALU.add)
+            nc.scalar.activation(g2[0, t][:, cols], g2[0, t][:, cols], ACT.Abs)
+
+        turned = [(1, t) for t in range(PACK)]
+        prod_T = [held([P, BANK], F32, f"prod_T{b}", tag=f"small{b}") for b in range(S // P)]
+        bench_T = {
+            (s, j): (
+                laid([P, BANK], F32, f"bench_T{n}{j}", 9 + 2 * j)
+                if s == turned[-1]
+                else held([P, BANK], F32, f"bench_T{n}{j}")
+            )
+            for n, s in enumerate(turned)
+            for j in range(halves)
+        }
+
+        def turned_product(b, where):
+            j, c0 = b // PACK, (b % PACK) * P
+            acc = bank(where)
+            nc.tensor.matmul_mx(
+                out=acc[:],
+                lhsT=h_c[j][:, c0 : c0 + P].bitcast(FP8X4),
+                lhsT_scale=h_sc[j][:, c0 : c0 + P],
+                rhs=w3_raw[:, BANK : 2 * BANK].bitcast(FP8X4),
+                rhs_scale=w3_sc_raw[:, BANK : 2 * BANK],
+                start=True,
+                stop=True,
+            )
+            nc.scalar.copy(
+                prod_T[b][:].rearrange("j (t q) -> j t q", t=PACK), acc[:].rearrange("j (q t) -> j t q", t=PACK)
+            )
+
+        def turned_bench(s, j, where):
+            acc = bank(where)
+            for c0 in range(0, BANK, P):
+                block = bench_t[s[0]][:, s[1], j * BANK + c0 : j * BANK + c0 + P]
+                nc.tensor.transpose(acc[:, c0 : c0 + P], block, ident[:])
+            nc.scalar.copy(bench_T[s, j][:], acc[:])
+
+        def turned_back(s, j, where):
+            acc = bank(where)
+            g, t = s
+            for c in range(PACK):
+                cols = slice(c * P, (c + 1) * P)
+                prod = prod_T[j * PACK + c][:, t * P : (t + 1) * P]
+                for n, term in enumerate((prod, bench_T[s, j][:, cols])):
+                    nc.tensor.matmul(acc[:, cols], term, ident[:], start=(n == 0), stop=(n == 1), is_transpose=True)
+            nc.scalar.activation(g2[s][:, j * BANK : (j + 1) * BANK], acc[:], ACT.Abs)
 
         y = [held([P, PACK, M], F32, f"y{g}") for g in range(groups)]
-        y_b = [held([P, PACK * M], BF16, f"y_b{g}") for g in range(groups)]
         y_c = [held([P, M], I32, f"y_c{g}") for g in range(groups)]
         y_sc = held([P, groups * M], U8, "y_sc")
         pair = {}
@@ -223,7 +277,6 @@ def tile_list_reed_pair_card_kernel(
                 nc.vector.tensor_copy(
                     both[:, n * width : (n + 1) * width], g2[g, t][:].indirect(pos_t[:, m0 // 16 : m1 // 16])
                 )
-            nc.scalar.activation(both[:, 0 : 2 * width], both[:, 0 : 2 * width], ACT.Abs)
             pair[g, t, m0] = both
 
         def larger(g, t, m0, m1):
@@ -249,20 +302,30 @@ def tile_list_reed_pair_card_kernel(
                 out_1[g].rearrange("p m t -> p (m t)").bitcast(I32)[:, m0:m1], y_c[g][:, m0:m1]
             )
 
+        for n, s in enumerate(turned[0:2]):
+            for j in range(halves):
+                turned_bench(s, j, halves * n + j)
+        for j in range(halves):
+            for t in range(PACK):
+                direct(j, t)
+        for b in range(S // P):
+            turned_product(b, (b + PACK) % 8)
+        for s, back, ahead in ((turned[0], 4, None), (turned[1], 6, None), (turned[2], 2, 0), (turned[3], 6, 4)):
+            for j in range(halves):
+                if ahead is not None:
+                    turned_bench(s, j, ahead + j)
+                turned_back(s, j, back + j)
+        y_b = [laid([P, PACK * M], BF16, "y_b0", 9), held([P, PACK * M], BF16, "y_b1")]
+
         steps = [(g, t, 0, M) for g, t in slices[:-1]]
         steps.extend([slices[-1] + (0, M // 2), slices[-1] + (M // 2, M)])
-        for g, t in slices:
-            second(0, g, t)
-        second(1, *slices[0])
         for n, s in enumerate(steps):
-            if n + 1 < len(slices):
-                second(1, *slices[n + 1])
             pick(*s)
             if n > 0:
                 larger(*steps[n - 1])
             if n == PACK:
                 weave(nc.scalar.copy, 0, 0, M)
-            if n == PACK + 2:
+            if n == len(steps) - 2:
                 planes(0, 0, M)
         weave(nc.scalar.copy, 1, 0, M // 2)
         larger(*steps[-1])

@@ -19,8 +19,38 @@ ACT = mybir.ActivationFunctionType
 
 P = 128
 PACK = 4
+SPAN = P * PACK
 BANK = 512
-QUADS = 4
+QUAD = 32
+QUADS = P // QUAD
+ROWS = 4
+PER_COL = 16
+LINE = 16
+PASSES = K // SPAN
+HALVES = S // BANK
+GROUPS = N // SPAN
+
+AT_W1 = (0, 9)
+AT_W3_SCALES = 8
+AT_TAB_SCALES = 7
+AT_TAB_WORDS = (17, 33)
+AT_W3_WORDS = 17
+AT_BENCH = (21, 37)
+AT_Y_WOVEN = 9
+
+
+def deal(nc, out, in_, run):
+    nc.vector.tensor_copy(
+        out.rearrange("p (a t c i) -> p a c t i", t=PACK, c=P // run, i=run),
+        in_.rearrange("p (a c i t) -> p a c t i", t=PACK, c=P // run, i=run),
+    )
+
+
+def weave(copy, out, in_):
+    copy(
+        out.rearrange("p (c i t) -> p c t i", i=4, t=PACK),
+        in_.rearrange("p t (c i) -> p c t i", i=4),
+    )
 
 
 def tile_list_reed_pair_card_kernel(
@@ -28,9 +58,6 @@ def tile_list_reed_pair_card_kernel(
     w3_words, w3_scales, bench, pos1, pos2, out_0, out_1, out_2,
 ):
     nc = tc.nc
-    passes = K // (P * PACK)
-    halves = S // BANK
-    groups = N // (P * PACK)
 
     with ExitStack() as ctx:
         keep = ctx.enter_context(tc.tile_pool(name="keep", bufs=1))
@@ -47,11 +74,11 @@ def tile_list_reed_pair_card_kernel(
         def bank(b):
             return psum.tile([P, BANK], F32, name=f"bank{b}")
 
-        offs_t = held([P, S // 16], U16, "offs_t")
-        pos1_t = held([P, M // 16], U16, "pos1_t")
-        pos2_t = held([P, M // 16], U16, "pos2_t")
-        tab_sc = laid([P, T], U8, "tab_sc", 7)
-        w2_sc_raw = held([P, passes * H], U8, "w2_sc_raw")
+        offs_t = held([P, S // PER_COL], U16, "offs_t")
+        pos1_t = held([P, M // PER_COL], U16, "pos1_t")
+        pos2_t = held([P, M // PER_COL], U16, "pos2_t")
+        tab_sc = laid([P, T], U8, "tab_sc", AT_TAB_SCALES)
+        w2_sc_raw = held([P, PASSES * H], U8, "w2_sc_raw")
         v_sc1 = held([P, S], U8, "v_sc1")
         nc.vector.memset(tab_sc[:, 0 : T // 2].bitcast(I32), 0)
         nc.gpsimd.memset(tab_sc[:, T // 2 : T].bitcast(I32), 0)
@@ -61,236 +88,238 @@ def tile_list_reed_pair_card_kernel(
         make_identity(nc, ident[:])
 
         nc.sync.dma_start(offs_t[:], offs)
-        w2_raw = held([P, passes * H // 2], I32, "w2_raw")
+        w2_raw = held([P, PASSES * H // 2], I32, "w2_raw")
         nc.sync.dma_start(
-            w2_raw[:].rearrange("p (a c) -> p a c", a=passes),
+            w2_raw[:].rearrange("p (a c) -> p a c", a=PASSES),
             w2_words.bitcast(I32).rearrange("a p c -> p a c"),
         )
         gain_t = held([P, PACK], F32, "gain_t")
         nc.sync.dma_start(gain_t[:], gain.rearrange("(p t) -> p t", t=PACK))
         for q in range(QUADS):
             nc.sync.dma_start(
-                tab_sc[32 * q : 32 * q + 4 * passes, :].bitcast(I32),
-                tab_scales[:, 4 * q : 4 * q + 4, :].bitcast(I32),
+                tab_sc[QUAD * q : QUAD * q + ROWS * PASSES, :].bitcast(I32),
+                tab_scales[:, ROWS * q : ROWS * (q + 1), :].bitcast(I32),
             )
-        tab_w = [laid([P, T], I32, f"tab_w{a}", 17 + 16 * a) for a in range(passes)]
+        tab_w = [laid([P, T], I32, f"tab_w{a}", AT_TAB_WORDS[a]) for a in range(PASSES)]
         nc.sync.dma_start(tab_w[0][:], tab_words[0].rearrange("p n i -> p (n i)").bitcast(I32))
-        for q in range(QUADS):
+        for r in range(ROWS):
             nc.sync.dma_start(
-                w2_sc_raw[q:P:32, :].bitcast(I32).rearrange("r (a c) -> r a c", a=passes),
-                w2_scales[:, q:16:4, :].bitcast(I32).rearrange("a r c -> r a c"),
+                w2_sc_raw[r:P:QUAD, :].bitcast(I32).rearrange("q (a c) -> q a c", a=PASSES),
+                w2_scales[:, r : ROWS * QUADS : ROWS, :].bitcast(I32).rearrange("a q c -> q a c"),
             )
         nc.sync.dma_start(tab_w[1][:], tab_words[1].rearrange("p n i -> p (n i)").bitcast(I32))
         nc.sync.dma_start(pos1_t[:], pos1)
         nc.sync.dma_start(pos2_t[:], pos2)
 
-        warm = held([P, PACK], F32, "warm")
-        nc.scalar.activation(warm[:], gain_t[:], ACT.Tanh)
-
-        w2_c = held([P, passes * H], U16, "w2_c")
-        nc.vector.tensor_copy(
-            w2_c[:].rearrange("p (a t q) -> p a q t", a=passes, t=PACK),
-            w2_raw[:].bitcast(U16).rearrange("p (a q t) -> p a q t", a=passes, t=PACK),
-        )
-        v_c = [[held([P, BANK], U32, f"v_c{a}{j}") for j in range(halves)] for a in range(passes)]
-        w2_sc = held([P, passes * H], U8, "w2_sc")
-        cols16 = BANK // 16
+        w2_c = held([P, PASSES * H], U16, "w2_c")
+        deal(nc, w2_c[:], w2_raw[:].bitcast(U16), LINE // 2)
         v_sc0 = held([P, S], U8, "v_sc0")
         nc.vector.tensor_copy(v_sc0[:], tab_sc[:].indirect(offs_t[:]))
-        for q in range(QUADS):
-            nc.sync.dma_start(v_sc1[q:P:32, :].bitcast(I32), v_sc0[4 + q : P : 32, :].bitcast(I32))
+        for r in range(ROWS):
+            nc.sync.dma_start(v_sc1[r:P:QUAD, :].bitcast(I32), v_sc0[ROWS + r : P : QUAD, :].bitcast(I32))
         v_sc = [v_sc0, v_sc1]
-        w1_raw = [laid([P, PACK, H], F32, f"w1_raw{a}", 9 * a) for a in range(passes)]
-        for a in range(passes):
+
+        w1_raw = [laid([P, PACK, H], F32, f"w1_raw{a}", AT_W1[a]) for a in range(PASSES)]
+        for a in range(PASSES):
             nc.sync.dma_start(
-                w1_raw[a][:], w1[a * 512 : (a + 1) * 512, :].rearrange("(p i) c -> p i c", i=PACK)
+                w1_raw[a][:], w1[a * SPAN : (a + 1) * SPAN, :].rearrange("(p i) c -> p i c", i=PACK)
             )
-        w3_sc_raw = laid([P, N], U8, "w3_sc_raw", 8)
+        w3_sc_raw = laid([P, N], U8, "w3_sc_raw", AT_W3_SCALES)
         nc.gpsimd.memset(w3_sc_raw[:].bitcast(I32), 0)
-        for q in range(QUADS):
-            nc.sync.dma_start(w3_sc_raw[q:P:32, :].bitcast(I32), w3_scales[0, q:16:4, :].bitcast(I32))
-        for a in range(passes):
-            for j in range(halves):
-                nc.vector.tensor_copy(
-                    v_c[a][j][:],
-                    tab_w[a][:].bitcast(U32).indirect(offs_t[:, j * cols16 : (j + 1) * cols16]),
-                )
-                if a == 0:
-                    cols = slice(j * H, (j + 1) * H)
-                    nc.vector.tensor_copy(
-                        w2_sc[:, cols].rearrange("p (t q) -> p q t", t=PACK),
-                        w2_sc_raw[:, cols].rearrange("p (q t) -> p q t", t=PACK),
-                    )
-        w3_raw = laid([P, N], I32, "w3_raw", 17)
-        nc.sync.dma_start(w3_raw[:], w3_words[0].rearrange("p n i -> p (n i)").bitcast(I32))
-
-        bench_t = [laid([P, PACK, S], F32, f"bench{g}", 37 - 16 * g) for g in range(groups)]
-        for g in reversed(range(groups)):
+        for r in range(ROWS):
             nc.sync.dma_start(
-                bench_t[g][:], bench[g * 512 : (g + 1) * 512, :].rearrange("(p t) j -> p t j", t=PACK)
+                w3_sc_raw[r:P:QUAD, :].bitcast(I32), w3_scales[0, r : ROWS * QUADS : ROWS, :].bitcast(I32)
             )
 
-        units = [(j, t) for j in range(halves) for t in range(PACK)]
-        ordered = [(j, a, t) for j in range(halves) for a in range(passes) for t in range(PACK)]
-        bend = {u: bank(n) for n, u in enumerate(units)}
+        v_c = [[held([P, BANK], U32, f"v_c{a}{j}") for j in range(HALVES)] for a in range(PASSES)]
+        w2_sc = held([P, PASSES * H], U8, "w2_sc")
+
+        def gather_words(a, j):
+            entries = offs_t[:, j * BANK // PER_COL : (j + 1) * BANK // PER_COL]
+            nc.vector.tensor_copy(v_c[a][j][:], tab_w[a][:].bitcast(U32).indirect(entries))
+
+        def deal_w2_scales(a):
+            deal(nc, w2_sc[:, a * H : (a + 1) * H], w2_sc_raw[:, a * H : (a + 1) * H], LINE)
+
+        gather_words(0, 0)
+        deal_w2_scales(0)
+        gather_words(0, 1)
+        deal_w2_scales(1)
+        gather_words(1, 0)
+        gather_words(1, 1)
+
+        w3_raw = laid([P, N], I32, "w3_raw", AT_W3_WORDS)
+        nc.sync.dma_start(w3_raw[:], w3_words[0].rearrange("p n i -> p (n i)").bitcast(I32))
+        bench_t = [laid([P, PACK, S], F32, f"bench{g}", AT_BENCH[g]) for g in range(GROUPS)]
+        for g in range(GROUPS):
+            nc.sync.dma_start(
+                bench_t[g][:], bench[g * SPAN : (g + 1) * SPAN, :].rearrange("(p t) j -> p t j", t=PACK)
+            )
+
+        units = [(j, t) for j in range(HALVES) for t in range(PACK)]
+        bend = {u: bank(b) for b, u in enumerate(units)}
         w2_bytes = w2_c[:].bitcast(U8)
-        for j, a, t in ordered:
-            if True:
-                c0 = a * H + t * P
-                nc.tensor.matmul_mx(
-                    out=bend[j, t][:],
-                    lhsT=w2_bytes[:, 2 * c0 : 2 * (c0 + P)].bitcast(FP4X4),
-                    lhsT_scale=w2_sc[:, c0 : c0 + P],
-                    rhs=v_c[a][j][:].bitcast(FP8X4),
-                    rhs_scale=v_sc[a][:, j * BANK : (j + 1) * BANK],
-                    start=(a == 0),
-                    stop=(a == passes - 1),
-                )
-        bent = {u: held([P, BANK], F32, f"bent{n}", tag=f"small{n}") for n, u in enumerate(units)}
-        for j in range(halves):
+        for j in range(HALVES):
+            for a in range(PASSES):
+                for t in range(PACK):
+                    c0 = a * H + t * P
+                    nc.tensor.matmul_mx(
+                        out=bend[j, t][:],
+                        lhsT=w2_bytes[:, 2 * c0 : 2 * (c0 + P)].bitcast(FP4X4),
+                        lhsT_scale=w2_sc[:, c0 : c0 + P],
+                        rhs=v_c[a][j][:].bitcast(FP8X4),
+                        rhs_scale=v_sc[a][:, j * BANK : (j + 1) * BANK],
+                        start=(a == 0),
+                        stop=(a == PASSES - 1),
+                    )
+        bent = {u: held([P, BANK], F32, f"bent{b}", tag=f"unit{b}") for b, u in enumerate(units)}
+        for j in range(HALVES):
             for t in range(PACK):
                 nc.scalar.activation(bent[j, t][:], bend[j, t][:], ACT.Tanh)
             for t in range(PACK):
                 nc.scalar.activation(bent[j, t][:], bent[j, t][:], ACT.Copy, scale=gain_t[:, t : t + 1])
 
-        w1_c = [held([P, H], U32, f"w1_c{a}") for a in range(passes)]
-        w1_sc = [held([P, H], U8, f"w1_sc{a}") for a in range(passes)]
-        w1_b = [held([P, PACK * H], BF16, f"w1_b{a}") for a in range(passes)]
-        for a in range(passes):
+        w1_c = [held([P, H], U32, f"w1_c{a}") for a in range(PASSES)]
+        w1_sc = [held([P, H], U8, f"w1_sc{a}") for a in range(PASSES)]
+        w1_b = [held([P, PACK * H], BF16, f"w1_b{a}") for a in range(PASSES)]
+        for a in range(PASSES):
             nc.vector.tensor_copy(
-                w1_b[a][:].rearrange("p (t q i) -> p q i t", t=PACK, i=PACK),
-                w1_raw[a][:].rearrange("p i (q t) -> p q i t", t=PACK),
+                w1_b[a][:].rearrange("p (t q i) -> p q t i", t=PACK, i=PACK),
+                w1_raw[a][:].rearrange("p i (q t) -> p q t i", t=PACK),
             )
             nc.vector.quantize_mx(out=w1_c[a][:].bitcast(FP8X4), scales=w1_sc[a][:], in_=w1_b[a][:])
 
-        lin = {u: bank(n) for n, u in enumerate(units)}
-        for j, n, t in ordered:
-            for a in [n if j == 0 else passes - 1 - n]:
-                nc.tensor.matmul_mx(
-                    out=lin[j, t][:],
-                    lhsT=w1_c[a][:, t * P : (t + 1) * P].bitcast(FP8X4),
-                    lhsT_scale=w1_sc[a][:, t * P : (t + 1) * P],
-                    rhs=v_c[a][j][:].bitcast(FP8X4),
-                    rhs_scale=v_sc[a][:, j * BANK : (j + 1) * BANK],
-                    start=(n == 0),
-                    stop=(n == passes - 1),
-                )
+        lin = {u: bank(b) for b, u in enumerate(units)}
+        for j, order in enumerate(((0, 1), (1, 0))):
+            for a in order:
+                for t in range(PACK):
+                    nc.tensor.matmul_mx(
+                        out=lin[j, t][:],
+                        lhsT=w1_c[a][:, t * P : (t + 1) * P].bitcast(FP8X4),
+                        lhsT_scale=w1_sc[a][:, t * P : (t + 1) * P],
+                        rhs=v_c[a][j][:].bitcast(FP8X4),
+                        rhs_scale=v_sc[a][:, j * BANK : (j + 1) * BANK],
+                        start=(a == order[0]),
+                        stop=(a == order[-1]),
+                    )
 
-        h_rows = [held([P, PACK, BANK], BF16, f"h_rows{j}") for j in range(halves)]
-        h_b = [held([P, PACK * BANK], BF16, f"h_b{j}") for j in range(halves)]
-        h_c = [held([P, BANK], U32, f"h_c{j}") for j in range(halves)]
-        h_sc = [held([P, BANK], U8, f"h_sc{j}") for j in range(halves)]
-        w3_c = held([P, BANK], I32, "w3_c")
-        nc.vector.tensor_copy(
-            w3_c[:].rearrange("p (t q) -> p q t", t=PACK),
-            w3_raw[:, 0:BANK].rearrange("p (q t) -> p q t", t=PACK),
-        )
-        w3_sc = held([P, BANK], U8, "w3_sc")
-        nc.vector.tensor_copy(
-            w3_sc[:].rearrange("p (t q) -> p q t", t=PACK),
-            w3_sc_raw[:, 0:BANK].rearrange("p (q t) -> p q t", t=PACK),
-        )
+        w3_c = held([P, SPAN], I32, "w3_c")
+        deal(nc, w3_c[:], w3_raw[:, 0:SPAN], LINE // 4)
+        w3_sc = held([P, SPAN], U8, "w3_sc")
+        deal(nc, w3_sc[:], w3_sc_raw[:, 0:SPAN], LINE)
 
+        h_rows = [held([P, PACK, BANK], BF16, f"h_rows{j}") for j in range(HALVES)]
+        h_b = [held([P, PACK * BANK], BF16, f"h_b{j}") for j in range(HALVES)]
+        h_c = [held([P, BANK], U32, f"h_c{j}") for j in range(HALVES)]
+        h_sc = [held([P, BANK], U8, f"h_sc{j}") for j in range(HALVES)]
         for j, copy in enumerate((nc.vector.tensor_copy, nc.scalar.copy)):
             for t in range(PACK):
                 nc.vector.scalar_tensor_tensor(
                     h_rows[j][:, t, :], lin[j, t][:], gain_t[:, t : t + 1], bent[j, t][:], ALU.mult, ALU.add
                 )
-            copy(
-                h_b[j][:].rearrange("p (c i t) -> p c t i", i=4, t=PACK),
-                h_rows[j][:].rearrange("p t (c i) -> p c t i", i=4),
-            )
+            weave(copy, h_b[j][:], h_rows[j][:])
             nc.vector.quantize_mx(out=h_c[j][:].bitcast(FP8X4), scales=h_sc[j][:], in_=h_b[j][:])
 
-        slices = [(g, t) for g in range(groups) for t in range(PACK)]
-        g2 = {s: held([P, S], F32, f"g2_{s[0]}{s[1]}") for s in slices}
+        size = {(g, t): held([P, S], F32, f"size{g}{t}") for g in range(GROUPS) for t in range(PACK)}
+
         def direct(j, t):
-            c0 = t * P
             acc = bank(j * PACK + t)
             nc.tensor.matmul_mx(
                 out=acc[:],
-                lhsT=w3_c[:, c0 : c0 + P].bitcast(FP8X4),
-                lhsT_scale=w3_sc[:, c0 : c0 + P],
+                lhsT=w3_c[:, t * P : (t + 1) * P].bitcast(FP8X4),
+                lhsT_scale=w3_sc[:, t * P : (t + 1) * P],
                 rhs=h_c[j][:].bitcast(FP8X4),
                 rhs_scale=h_sc[j][:],
                 start=True,
                 stop=True,
             )
             cols = slice(j * BANK, (j + 1) * BANK)
-            nc.vector.tensor_tensor(g2[0, t][:, cols], acc[:], bench_t[0][:, t, cols], ALU.add)
-            nc.scalar.activation(g2[0, t][:, cols], g2[0, t][:, cols], ACT.Abs)
+            nc.vector.tensor_tensor(size[0, t][:, cols], acc[:], bench_t[0][:, t, cols], ALU.add)
+            nc.scalar.activation(size[0, t][:, cols], size[0, t][:, cols], ACT.Abs)
 
-        turned = [(1, t) for t in range(PACK)]
-        prod_T = [held([P, BANK], F32, f"prod_T{b}", tag=f"small{b}") for b in range(S // P)]
+        prod_T = [held([P, SPAN], F32, f"prod_T{b}", tag=f"unit{b}") for b in range(S // P)]
         bench_T = {
-            (s, j): (
-                laid([P, BANK], F32, f"bench_T{n}{j}", 9 + 2 * j)
-                if s == turned[-1]
-                else held([P, BANK], F32, f"bench_T{n}{j}")
+            (t, j): (
+                laid([P, BANK], F32, f"bench_T{t}{j}", AT_Y_WOVEN + 2 * j)
+                if t == 1
+                else held([P, BANK], F32, f"bench_T{t}{j}")
             )
-            for n, s in enumerate(turned)
-            for j in range(halves)
+            for t in range(PACK)
+            for j in range(HALVES)
         }
 
-        def turned_product(b, where):
-            j, c0 = b // PACK, (b % PACK) * P
-            acc = bank(where)
+        def turned_product(j, c):
+            acc = bank(PACK + c)
             nc.tensor.matmul_mx(
                 out=acc[:],
-                lhsT=h_c[j][:, c0 : c0 + P].bitcast(FP8X4),
-                lhsT_scale=h_sc[j][:, c0 : c0 + P],
-                rhs=w3_raw[:, BANK : 2 * BANK].bitcast(FP8X4),
-                rhs_scale=w3_sc_raw[:, BANK : 2 * BANK],
+                lhsT=h_c[j][:, c * P : (c + 1) * P].bitcast(FP8X4),
+                lhsT_scale=h_sc[j][:, c * P : (c + 1) * P],
+                rhs=w3_raw[:, SPAN : 2 * SPAN].bitcast(FP8X4),
+                rhs_scale=w3_sc_raw[:, SPAN : 2 * SPAN],
                 start=True,
                 stop=True,
             )
             nc.scalar.copy(
-                prod_T[b][:].rearrange("j (t q) -> j t q", t=PACK), acc[:].rearrange("j (q t) -> j t q", t=PACK)
+                prod_T[j * PACK + c][:].rearrange("p (t q) -> p t q", t=PACK),
+                acc[:].rearrange("p (q t) -> p t q", t=PACK),
             )
 
-        def turned_bench(s, j, where):
+        def turned_bench(t, j, where):
             acc = bank(where)
             for c0 in range(0, BANK, P):
-                block = bench_t[s[0]][:, s[1], j * BANK + c0 : j * BANK + c0 + P]
+                block = bench_t[1][:, t, j * BANK + c0 : j * BANK + c0 + P]
                 nc.tensor.transpose(acc[:, c0 : c0 + P], block, ident[:])
-            nc.scalar.copy(bench_T[s, j][:], acc[:])
+            nc.scalar.copy(bench_T[t, j][:], acc[:])
 
-        def turned_back(s, j, where):
+        def turned_back(t, j, where):
             acc = bank(where)
-            g, t = s
             for c in range(PACK):
                 cols = slice(c * P, (c + 1) * P)
                 prod = prod_T[j * PACK + c][:, t * P : (t + 1) * P]
-                for n, term in enumerate((prod, bench_T[s, j][:, cols])):
-                    nc.tensor.matmul(acc[:, cols], term, ident[:], start=(n == 0), stop=(n == 1), is_transpose=True)
-            nc.scalar.activation(g2[s][:, j * BANK : (j + 1) * BANK], acc[:], ACT.Abs)
+                nc.tensor.matmul(acc[:, cols], prod, ident[:], start=True, stop=False, is_transpose=True)
+                nc.tensor.matmul(
+                    acc[:, cols], bench_T[t, j][:, cols], ident[:], start=False, stop=True, is_transpose=True
+                )
+            nc.scalar.activation(size[1, t][:, j * BANK : (j + 1) * BANK], acc[:], ACT.Abs)
 
-        y = [held([P, PACK, M], F32, f"y{g}") for g in range(groups)]
-        y_c = [held([P, M], I32, f"y_c{g}") for g in range(groups)]
-        y_sc = held([P, groups * M], U8, "y_sc")
-        pair = {}
+        for j, t in units:
+            direct(j, t)
+        early = PACK // 2
+        for t in range(early):
+            for j in range(HALVES):
+                turned_bench(t, j, HALVES * t + j)
+        for j in range(HALVES):
+            for c in range(PACK):
+                turned_product(j, c)
+        for t in range(PACK):
+            for j in range(HALVES):
+                if t >= early:
+                    turned_bench(t, j, HALVES * (t - early) + j)
+                turned_back(t, j, HALVES * t + j)
+
+        y = [held([P, PACK, M], F32, f"y{g}") for g in range(GROUPS)]
+        y_b = [laid([P, PACK * M], BF16, "y_b0", AT_Y_WOVEN), held([P, PACK * M], BF16, "y_b1")]
+        y_c = [held([P, M], I32, f"y_c{g}") for g in range(GROUPS)]
+        y_sc = held([P, GROUPS * M], U8, "y_sc")
+        picked = {}
 
         def pick(g, t, m0, m1):
             width = m1 - m0
             both = ring.tile([P, 2 * M], F32, name="both")
-            for n, pos_t in enumerate((pos1_t, pos2_t)):
-                nc.vector.tensor_copy(
-                    both[:, n * width : (n + 1) * width], g2[g, t][:].indirect(pos_t[:, m0 // 16 : m1 // 16])
-                )
-            pair[g, t, m0] = both
+            for side, pos_t in enumerate((pos1_t, pos2_t)):
+                entries = pos_t[:, m0 // PER_COL : m1 // PER_COL]
+                nc.vector.tensor_copy(both[:, side * width : (side + 1) * width], size[g, t][:].indirect(entries))
+            picked[g, t, m0] = both
 
         def larger(g, t, m0, m1):
             width = m1 - m0
-            both = pair[g, t, m0]
+            both = picked[g, t, m0]
             nc.vector.tensor_tensor(y[g][:, t, m0:m1], both[:, 0:width], both[:, width : 2 * width], ALU.max)
-            rows = out_0[g * 512 : (g + 1) * 512, :].rearrange("(p t) m -> p t m", t=PACK)
+            rows = out_0[g * SPAN : (g + 1) * SPAN, :].rearrange("(p t) m -> p t m", t=PACK)
             nc.sync.dma_start(rows[:, t, m0:m1], y[g][:, t, m0:m1])
 
-        def weave(copy, g, m0, m1):
-            copy(
-                y_b[g][:, PACK * m0 : PACK * m1].rearrange("p (c i t) -> p c t i", i=4, t=PACK),
-                y[g][:, :, m0:m1].rearrange("p t (c i) -> p c t i", i=4),
-            )
+        def weave_y(copy, g, m0, m1):
+            weave(copy, y_b[g][:, PACK * m0 : PACK * m1], y[g][:, :, m0:m1])
 
         def planes(g, m0, m1):
             nc.vector.quantize_mx(
@@ -298,42 +327,26 @@ def tile_list_reed_pair_card_kernel(
                 scales=y_sc[:, g * M + m0 : g * M + m1],
                 in_=y_b[g][:, PACK * m0 : PACK * m1],
             )
-            nc.sync.dma_start(
-                out_1[g].rearrange("p m t -> p (m t)").bitcast(I32)[:, m0:m1], y_c[g][:, m0:m1]
-            )
+            nc.sync.dma_start(out_1[g].rearrange("p m t -> p (m t)").bitcast(I32)[:, m0:m1], y_c[g][:, m0:m1])
 
-        for n, s in enumerate(turned[0:2]):
-            for j in range(halves):
-                turned_bench(s, j, halves * n + j)
-        for j in range(halves):
-            for t in range(PACK):
-                direct(j, t)
-        for b in range(S // P):
-            turned_product(b, (b + PACK) % 8)
-        for s, back, ahead in ((turned[0], 4, None), (turned[1], 6, None), (turned[2], 2, 0), (turned[3], 6, 4)):
-            for j in range(halves):
-                if ahead is not None:
-                    turned_bench(s, j, ahead + j)
-                turned_back(s, j, back + j)
-        y_b = [laid([P, PACK * M], BF16, "y_b0", 9), held([P, PACK * M], BF16, "y_b1")]
-
-        steps = [(g, t, 0, M) for g, t in slices[:-1]]
-        steps.extend([slices[-1] + (0, M // 2), slices[-1] + (M // 2, M)])
-        for n, s in enumerate(steps):
-            pick(*s)
+        mid = M // 2
+        steps = [(g, t, 0, M) for g in range(GROUPS) for t in range(PACK)][:-1]
+        steps.extend([(1, PACK - 1, 0, mid), (1, PACK - 1, mid, M)])
+        for n, step in enumerate(steps):
+            pick(*step)
             if n > 0:
                 larger(*steps[n - 1])
             if n == PACK:
-                weave(nc.scalar.copy, 0, 0, M)
+                weave_y(nc.scalar.copy, 0, 0, M)
             if n == len(steps) - 2:
                 planes(0, 0, M)
-        weave(nc.scalar.copy, 1, 0, M // 2)
+        weave_y(nc.scalar.copy, 1, 0, mid)
         larger(*steps[-1])
-        weave(nc.vector.tensor_copy, 1, M // 2, M)
-        planes(1, 0, M // 2)
-        planes(1, M // 2, M)
+        weave_y(nc.vector.tensor_copy, 1, mid, M)
+        planes(1, 0, mid)
+        planes(1, mid, M)
         for q in range(QUADS):
             nc.scalar.dma_start(
-                out_2[:, 4 * q : 4 * q + 4, :].bitcast(I32).rearrange("g r m -> r g m"),
-                y_sc[32 * q : 32 * q + 4, :].bitcast(I32).rearrange("r (g m) -> r g m", g=groups),
+                out_2[:, ROWS * q : ROWS * (q + 1), :].bitcast(I32).rearrange("g r m -> r g m"),
+                y_sc[QUAD * q : QUAD * q + ROWS, :].bitcast(I32).rearrange("r (g m) -> r g m", g=GROUPS),
             )

from contextlib import ExitStack

import concourse.mybir as mybir
from concourse.masks import make_identity

K, H, N, T, S, M = 1024, 512, 1024, 4096, 1024, 512
FLOPS = 2 * (2 * K * H * S + H * N * S)

F32 = mybir.dt.float32
BF16 = mybir.dt.bfloat16
I32 = mybir.dt.int32
U32 = mybir.dt.uint32
U16 = mybir.dt.uint16
U8 = mybir.dt.uint8
FP8X4 = mybir.dt.float8_e4m3fn_x4
FP4X4 = mybir.dt.float4_e2m1fn_x4
ALU = mybir.AluOpType
ACT = mybir.ActivationFunctionType

P = 128
PACK = 4
SPAN = P * PACK
BANK = 512
QUAD = 32
QUADS = P // QUAD
ROWS = 4
PER_COL = 16
LINE = 16
PASSES = K // SPAN
HALVES = S // BANK
GROUPS = N // SPAN

AT_W1 = (0, 9)
AT_W3_SCALES = 8
AT_TAB_SCALES = 7
AT_TAB_WORDS = (17, 33)
AT_W3_WORDS = 17
AT_BENCH = (21, 37)
AT_Y_WOVEN = 9


def deal(nc, out, in_, run):
    nc.vector.tensor_copy(
        out.rearrange("p (a t c i) -> p a c t i", t=PACK, c=P // run, i=run),
        in_.rearrange("p (a c i t) -> p a c t i", t=PACK, c=P // run, i=run),
    )


def weave(copy, out, in_):
    copy(
        out.rearrange("p (c i t) -> p c t i", i=4, t=PACK),
        in_.rearrange("p t (c i) -> p c t i", i=4),
    )


def tile_list_reed_pair_card_kernel(
    tc, tab_words, tab_scales, offs, w1, w2_words, w2_scales, gain,
    w3_words, w3_scales, bench, pos1, pos2, out_0, out_1, out_2,
):
    nc = tc.nc

    with ExitStack() as ctx:
        keep = ctx.enter_context(tc.tile_pool(name="keep", bufs=1))
        ring = ctx.enter_context(tc.tile_pool(name="ring", bufs=3))
        overlay = ctx.enter_context(tc.tile_pool(name="overlay", bufs=1))
        psum = ctx.enter_context(tc.psum_pool(name="psum", bufs=1))

        def held(shape, dtype, name, tag=None):
            return keep.tile(shape, dtype, name=name, tag=tag or name, align_bytes=64)

        def laid(shape, dtype, name, kib):
            return overlay.tile(shape, dtype, name=name, align_bytes=64, offset=kib * 1024)

        def bank(b):
            return psum.tile([P, BANK], F32, name=f"bank{b}")

        offs_t = held([P, S // PER_COL], U16, "offs_t")
        pos1_t = held([P, M // PER_COL], U16, "pos1_t")
        pos2_t = held([P, M // PER_COL], U16, "pos2_t")
        tab_sc = laid([P, T], U8, "tab_sc", AT_TAB_SCALES)
        w2_sc_raw = held([P, PASSES * H], U8, "w2_sc_raw")
        v_sc1 = held([P, S], U8, "v_sc1")
        nc.vector.memset(tab_sc[:, 0 : T // 2].bitcast(I32), 0)
        nc.gpsimd.memset(tab_sc[:, T // 2 : T].bitcast(I32), 0)
        nc.vector.memset(w2_sc_raw[:].bitcast(I32), 0)
        nc.gpsimd.memset(v_sc1[:].bitcast(I32), 0)
        ident = held([P, P], F32, "ident")
        make_identity(nc, ident[:])

        nc.sync.dma_start(offs_t[:], offs)
        w2_raw = held([P, PASSES * H // 2], I32, "w2_raw")
        nc.sync.dma_start(
            w2_raw[:].rearrange("p (a c) -> p a c", a=PASSES),
            w2_words.bitcast(I32).rearrange("a p c -> p a c"),
        )
        gain_t = held([P, PACK], F32, "gain_t")
        nc.sync.dma_start(gain_t[:], gain.rearrange("(p t) -> p t", t=PACK))
        for q in range(QUADS):
            nc.sync.dma_start(
                tab_sc[QUAD * q : QUAD * q + ROWS * PASSES, :].bitcast(I32),
                tab_scales[:, ROWS * q : ROWS * (q + 1), :].bitcast(I32),
            )
        tab_w = [laid([P, T], I32, f"tab_w{a}", AT_TAB_WORDS[a]) for a in range(PASSES)]
        nc.sync.dma_start(tab_w[0][:], tab_words[0].rearrange("p n i -> p (n i)").bitcast(I32))
        for r in range(ROWS):
            nc.sync.dma_start(
                w2_sc_raw[r:P:QUAD, :].bitcast(I32).rearrange("q (a c) -> q a c", a=PASSES),
                w2_scales[:, r : ROWS * QUADS : ROWS, :].bitcast(I32).rearrange("a q c -> q a c"),
            )
        nc.sync.dma_start(tab_w[1][:], tab_words[1].rearrange("p n i -> p (n i)").bitcast(I32))
        nc.sync.dma_start(pos1_t[:], pos1)
        nc.sync.dma_start(pos2_t[:], pos2)

        w2_c = held([P, PASSES * H], U16, "w2_c")
        deal(nc, w2_c[:], w2_raw[:].bitcast(U16), LINE // 2)
        v_sc0 = held([P, S], U8, "v_sc0")
        nc.vector.tensor_copy(v_sc0[:], tab_sc[:].indirect(offs_t[:]))
        for r in range(ROWS):
            nc.sync.dma_start(v_sc1[r:P:QUAD, :].bitcast(I32), v_sc0[ROWS + r : P : QUAD, :].bitcast(I32))
        v_sc = [v_sc0, v_sc1]

        w1_raw = [laid([P, PACK, H], F32, f"w1_raw{a}", AT_W1[a]) for a in range(PASSES)]
        for a in range(PASSES):
            nc.sync.dma_start(
                w1_raw[a][:], w1[a * SPAN : (a + 1) * SPAN, :].rearrange("(p i) c -> p i c", i=PACK)
            )
        w3_sc_raw = laid([P, N], U8, "w3_sc_raw", AT_W3_SCALES)
        nc.gpsimd.memset(w3_sc_raw[:].bitcast(I32), 0)
        for r in range(ROWS):
            nc.sync.dma_start(
                w3_sc_raw[r:P:QUAD, :].bitcast(I32), w3_scales[0, r : ROWS * QUADS : ROWS, :].bitcast(I32)
            )

        v_c = [[held([P, BANK], U32, f"v_c{a}{j}") for j in range(HALVES)] for a in range(PASSES)]
        w2_sc = held([P, PASSES * H], U8, "w2_sc")

        def gather_words(a, j):
            entries = offs_t[:, j * BANK // PER_COL : (j + 1) * BANK // PER_COL]
            nc.vector.tensor_copy(v_c[a][j][:], tab_w[a][:].bitcast(U32).indirect(entries))

        def deal_w2_scales(a):
            deal(nc, w2_sc[:, a * H : (a + 1) * H], w2_sc_raw[:, a * H : (a + 1) * H], LINE)

        gather_words(0, 0)
        deal_w2_scales(0)
        gather_words(0, 1)
        deal_w2_scales(1)
        gather_words(1, 0)
        gather_words(1, 1)

        w3_raw = laid([P, N], I32, "w3_raw", AT_W3_WORDS)
        nc.sync.dma_start(w3_raw[:], w3_words[0].rearrange("p n i -> p (n i)").bitcast(I32))
        bench_t = [laid([P, PACK, S], F32, f"bench{g}", AT_BENCH[g]) for g in range(GROUPS)]
        for g in range(GROUPS):
            nc.sync.dma_start(
                bench_t[g][:], bench[g * SPAN : (g + 1) * SPAN, :].rearrange("(p t) j -> p t j", t=PACK)
            )

        units = [(j, t) for j in range(HALVES) for t in range(PACK)]
        bend = {u: bank(b) for b, u in enumerate(units)}
        w2_bytes = w2_c[:].bitcast(U8)
        for j in range(HALVES):
            for a in range(PASSES):
                for t in range(PACK):
                    c0 = a * H + t * P
                    nc.tensor.matmul_mx(
                        out=bend[j, t][:],
                        lhsT=w2_bytes[:, 2 * c0 : 2 * (c0 + P)].bitcast(FP4X4),
                        lhsT_scale=w2_sc[:, c0 : c0 + P],
                        rhs=v_c[a][j][:].bitcast(FP8X4),
                        rhs_scale=v_sc[a][:, j * BANK : (j + 1) * BANK],
                        start=(a == 0),
                        stop=(a == PASSES - 1),
                    )
        bent = {u: held([P, BANK], F32, f"bent{b}", tag=f"unit{b}") for b, u in enumerate(units)}
        for j in range(HALVES):
            for t in range(PACK):
                nc.scalar.activation(bent[j, t][:], bend[j, t][:], ACT.Tanh)
            for t in range(PACK):
                nc.scalar.activation(bent[j, t][:], bent[j, t][:], ACT.Copy, scale=gain_t[:, t : t + 1])

        w1_c = [held([P, H], U32, f"w1_c{a}") for a in range(PASSES)]
        w1_sc = [held([P, H], U8, f"w1_sc{a}") for a in range(PASSES)]
        w1_b = [held([P, PACK * H], BF16, f"w1_b{a}") for a in range(PASSES)]
        for a in range(PASSES):
            nc.vector.tensor_copy(
                w1_b[a][:].rearrange("p (t q i) -> p q t i", t=PACK, i=PACK),
                w1_raw[a][:].rearrange("p i (q t) -> p q t i", t=PACK),
            )
            nc.vector.quantize_mx(out=w1_c[a][:].bitcast(FP8X4), scales=w1_sc[a][:], in_=w1_b[a][:])

        lin = {u: bank(b) for b, u in enumerate(units)}
        for j, order in enumerate(((0, 1), (1, 0))):
            for a in order:
                for t in range(PACK):
                    nc.tensor.matmul_mx(
                        out=lin[j, t][:],
                        lhsT=w1_c[a][:, t * P : (t + 1) * P].bitcast(FP8X4),
                        lhsT_scale=w1_sc[a][:, t * P : (t + 1) * P],
                        rhs=v_c[a][j][:].bitcast(FP8X4),
                        rhs_scale=v_sc[a][:, j * BANK : (j + 1) * BANK],
                        start=(a == order[0]),
                        stop=(a == order[-1]),
                    )

        w3_c = held([P, SPAN], I32, "w3_c")
        deal(nc, w3_c[:], w3_raw[:, 0:SPAN], LINE // 4)
        w3_sc = held([P, SPAN], U8, "w3_sc")
        deal(nc, w3_sc[:], w3_sc_raw[:, 0:SPAN], LINE)

        h_rows = [held([P, PACK, BANK], BF16, f"h_rows{j}") for j in range(HALVES)]
        h_b = [held([P, PACK * BANK], BF16, f"h_b{j}") for j in range(HALVES)]
        h_c = [held([P, BANK], U32, f"h_c{j}") for j in range(HALVES)]
        h_sc = [held([P, BANK], U8, f"h_sc{j}") for j in range(HALVES)]
        for j, copy in enumerate((nc.vector.tensor_copy, nc.scalar.copy)):
            for t in range(PACK):
                nc.vector.scalar_tensor_tensor(
                    h_rows[j][:, t, :], lin[j, t][:], gain_t[:, t : t + 1], bent[j, t][:], ALU.mult, ALU.add
                )
            weave(copy, h_b[j][:], h_rows[j][:])
            nc.vector.quantize_mx(out=h_c[j][:].bitcast(FP8X4), scales=h_sc[j][:], in_=h_b[j][:])

        size = {(g, t): held([P, S], F32, f"size{g}{t}") for g in range(GROUPS) for t in range(PACK)}

        def direct(j, t):
            acc = bank(j * PACK + t)
            nc.tensor.matmul_mx(
                out=acc[:],
                lhsT=w3_c[:, t * P : (t + 1) * P].bitcast(FP8X4),
                lhsT_scale=w3_sc[:, t * P : (t + 1) * P],
                rhs=h_c[j][:].bitcast(FP8X4),
                rhs_scale=h_sc[j][:],
                start=True,
                stop=True,
            )
            cols = slice(j * BANK, (j + 1) * BANK)
            nc.vector.tensor_tensor(size[0, t][:, cols], acc[:], bench_t[0][:, t, cols], ALU.add)
            nc.scalar.activation(size[0, t][:, cols], size[0, t][:, cols], ACT.Abs)

        prod_T = [held([P, SPAN], F32, f"prod_T{b}", tag=f"unit{b}") for b in range(S // P)]
        bench_T = {
            (t, j): (
                laid([P, BANK], F32, f"bench_T{t}{j}", AT_Y_WOVEN + 2 * j)
                if t == 1
                else held([P, BANK], F32, f"bench_T{t}{j}")
            )
            for t in range(PACK)
            for j in range(HALVES)
        }

        def turned_product(j, c):
            acc = bank(PACK + c)
            nc.tensor.matmul_mx(
                out=acc[:],
                lhsT=h_c[j][:, c * P : (c + 1) * P].bitcast(FP8X4),
                lhsT_scale=h_sc[j][:, c * P : (c + 1) * P],
                rhs=w3_raw[:, SPAN : 2 * SPAN].bitcast(FP8X4),
                rhs_scale=w3_sc_raw[:, SPAN : 2 * SPAN],
                start=True,
                stop=True,
            )
            nc.scalar.copy(
                prod_T[j * PACK + c][:].rearrange("p (t q) -> p t q", t=PACK),
                acc[:].rearrange("p (q t) -> p t q", t=PACK),
            )

        def turned_bench(t, j, where):
            acc = bank(where)
            for c0 in range(0, BANK, P):
                block = bench_t[1][:, t, j * BANK + c0 : j * BANK + c0 + P]
                nc.tensor.transpose(acc[:, c0 : c0 + P], block, ident[:])
            nc.scalar.copy(bench_T[t, j][:], acc[:])

        def turned_back(t, j, where):
            acc = bank(where)
            for c in range(PACK):
                cols = slice(c * P, (c + 1) * P)
                prod = prod_T[j * PACK + c][:, t * P : (t + 1) * P]
                nc.tensor.matmul(acc[:, cols], prod, ident[:], start=True, stop=False, is_transpose=True)
                nc.tensor.matmul(
                    acc[:, cols], bench_T[t, j][:, cols], ident[:], start=False, stop=True, is_transpose=True
                )
            nc.scalar.activation(size[1, t][:, j * BANK : (j + 1) * BANK], acc[:], ACT.Abs)

        for j, t in units:
            direct(j, t)
        early = PACK // 2
        for t in range(early):
            for j in range(HALVES):
                turned_bench(t, j, HALVES * t + j)
        for j in range(HALVES):
            for c in range(PACK):
                turned_product(j, c)
        for t in range(PACK):
            for j in range(HALVES):
                if t >= early:
                    turned_bench(t, j, HALVES * (t - early) + j)
                turned_back(t, j, HALVES * t + j)

        y = [held([P, PACK, M], F32, f"y{g}") for g in range(GROUPS)]
        y_b = [laid([P, PACK * M], BF16, "y_b0", AT_Y_WOVEN), held([P, PACK * M], BF16, "y_b1")]
        y_c = [held([P, M], I32, f"y_c{g}") for g in range(GROUPS)]
        y_sc = held([P, GROUPS * M], U8, "y_sc")
        picked = {}

        def pick(g, t, m0, m1):
            width = m1 - m0
            both = ring.tile([P, 2 * M], F32, name="both")
            for side, pos_t in enumerate((pos1_t, pos2_t)):
                entries = pos_t[:, m0 // PER_COL : m1 // PER_COL]
                nc.vector.tensor_copy(both[:, side * width : (side + 1) * width], size[g, t][:].indirect(entries))
            picked[g, t, m0] = both

        def larger(g, t, m0, m1):
            width = m1 - m0
            both = picked[g, t, m0]
            nc.vector.tensor_tensor(y[g][:, t, m0:m1], both[:, 0:width], both[:, width : 2 * width], ALU.max)
            rows = out_0[g * SPAN : (g + 1) * SPAN, :].rearrange("(p t) m -> p t m", t=PACK)
            nc.sync.dma_start(rows[:, t, m0:m1], y[g][:, t, m0:m1])

        def weave_y(copy, g, m0, m1):
            weave(copy, y_b[g][:, PACK * m0 : PACK * m1], y[g][:, :, m0:m1])

        def planes(g, m0, m1):
            nc.vector.quantize_mx(
                out=y_c[g][:, m0:m1].bitcast(FP8X4),
                scales=y_sc[:, g * M + m0 : g * M + m1],
                in_=y_b[g][:, PACK * m0 : PACK * m1],
            )
            nc.sync.dma_start(out_1[g].rearrange("p m t -> p (m t)").bitcast(I32)[:, m0:m1], y_c[g][:, m0:m1])

        mid = M // 2
        steps = [(g, t, 0, M) for g in range(GROUPS) for t in range(PACK)][:-1]
        steps.extend([(1, PACK - 1, 0, mid), (1, PACK - 1, mid, M)])
        for n, step in enumerate(steps):
            pick(*step)
            if n > 0:
                larger(*steps[n - 1])
            if n == PACK:
                weave_y(nc.scalar.copy, 0, 0, M)
            if n == len(steps) - 2:
                planes(0, 0, M)
        weave_y(nc.scalar.copy, 1, 0, mid)
        larger(*steps[-1])
        weave_y(nc.vector.tensor_copy, 1, mid, M)
        planes(1, 0, mid)
        planes(1, mid, M)
        for q in range(QUADS):
            nc.scalar.dma_start(
                out_2[:, ROWS * q : ROWS * (q + 1), :].bitcast(I32).rearrange("g r m -> r g m"),
                y_sc[QUAD * q : QUAD * q + ROWS, :].bitcast(I32).rearrange("r (g m) -> r g m", g=GROUPS),
            )
